import numpy as np
import ml_dtypes


def mxq(x, axis, fmt="e4m3"):
    dtype, down = {"e4m3": (ml_dtypes.float8_e4m3fn, 7), "e5m2": (ml_dtypes.float8_e5m2, 14)}[fmt]
    v = np.moveaxis(np.asarray(x, np.float32).astype(ml_dtypes.bfloat16).astype(np.float64), axis, -1)
    blocks = v.reshape(v.shape[:-1] + (-1, 32))
    amax = np.abs(blocks).max(-1, keepdims=True)
    byte = np.maximum(np.where(amax > 0, np.frexp(amax)[1] - 1 + 127, 0) - down, 1)
    scale = np.exp2(byte - 127.0)
    codes = (blocks / scale).astype(np.float32).astype(dtype).astype(np.float64)
    return np.moveaxis((codes * scale).reshape(v.shape), -1, axis)


WIDE = False


def mx_kscale(k):
    if not WIDE:
        return np.ones(k)
    levels = np.array([10, -10, 5, -5, 0])
    if k % 512:
        return np.exp2(np.random.permutation(np.resize(levels, k // 32))).repeat(32)
    a = np.empty((k // 512, 16))
    for p in range(k // 512):
        a[p, :8] = np.random.permutation(np.resize(levels, 8))
        for g in range(8):
            far = levels[np.abs(levels - a[p, g]) >= 10]
            a[p, g + 8] = far[np.random.randint(len(far))]
    return np.exp2(a.ravel()).repeat(32)


def f64(x):
    return np.asarray(x).astype(np.float64)


def striped(idx):
    return np.tile(np.asarray(idx).reshape(-1, 16).T, (8, 1)).astype(np.uint16)


def unstriped(offs):
    return offs[:16].T.reshape(-1).astype(np.int64)


E2M1 = np.array([0.0, 0.5, 1.0, 1.5, 2.0, 3.0, 4.0, 6.0, -0.0, -0.5, -1.0, -1.5, -2.0, -3.0, -4.0, -6.0])


def pack_weight(w, fmt):
    k, n = w.shape
    w = f64(np.asarray(w, np.float32).astype(ml_dtypes.bfloat16)).reshape(k // 32, 32, n)
    amax = np.abs(w).max(1)
    if fmt == "e4m3":
        byte = np.frexp(amax)[1] - 1 + 127 - 7
    else:
        mant, ex = np.frexp(amax / 6.0)
        byte = np.where(mant > 0.5, ex, ex - 1) + 127
    byte = np.clip(np.where(amax > 0, byte, 1), 1, 254)
    scaled = (w * np.exp2(127.0 - byte)[:, None, :]).reshape(k, n).astype(np.float32)
    by_word = np.ascontiguousarray(scaled.reshape(k // 512, 128, 4, n).transpose(0, 1, 3, 2))
    if fmt == "e4m3":
        words = by_word.astype(ml_dtypes.float8_e4m3fn).view(np.uint8)
    else:
        c = by_word.astype(ml_dtypes.float4_e2m1fn).view(np.uint8) & 0xF
        words = (c[..., 0::2] | (c[..., 1::2] << 4)).reshape(k // 512, 128, 2 * n)
    return np.ascontiguousarray(words), np.ascontiguousarray(byte.astype(np.uint8).reshape(k // 512, 16, n))


def unpack_weight(words, scales, fmt):
    g, _, n = scales.shape
    words = np.ascontiguousarray(words).reshape(g, 128, n, -1)
    if fmt == "e4m3":
        vals = words.view(ml_dtypes.float8_e4m3fn).astype(np.float64)
    else:
        nib = np.empty((g, 128, n, 4), np.uint8)
        nib[..., 0::2] = words & 0xF
        nib[..., 1::2] = words >> 4
        vals = E2M1[nib]
    vals = vals * np.repeat(np.exp2(scales.astype(np.float64) - 127.0), 8, axis=1)[..., None]
    return vals.transpose(0, 1, 3, 2).reshape(g * 512, n)


K, T, C, J, I, L, N = 512, 1024, 1024, 1024, 512, 512, 512


def setup_inputs():
    n = np.random.standard_normal
    idx = np.random.randint(0, C, J)
    idx2 = np.random.permutation(T)[:I]
    fk = mx_kscale(K)
    fj = mx_kscale(J)
    fl = mx_kscale(L)
    xtp = pack_weight(n((K, T)) / fk[:, None], "e4m3")
    wcp = pack_weight(n((K, C)) * 1 / np.sqrt(K) * fk[:, None], "e2m1")
    wop = pack_weight(n((J, N)) * 1 / np.sqrt(J) / fj[:, None], "e4m3")
    skp = pack_weight(n((L, I)) / fl[:, None], "e2m1")
    wsp = pack_weight(n((L, N)) * 1 / np.sqrt(L) * fl[:, None], "e4m3")
    return {
        "xt_words": xtp[0],
        "xt_scales": xtp[1],
        "wc_words": wcp[0],
        "wc_scales": wcp[1],
        "fj": (np.random.uniform(0.5, 2.0, (J, 1)) * fj[:, None]).astype(np.float32),
        "wo_words": wop[0],
        "wo_scales": wop[1],
        "sk_words": skp[0],
        "sk_scales": skp[1],
        "ws_words": wsp[0],
        "ws_scales": wsp[1],
        "offs": striped(idx),
        "offs2": striped(idx2),
    }


def reference(xt_words, xt_scales, wc_words, wc_scales, fj, wo_words, wo_scales, sk_words, sk_scales, ws_words, ws_scales, offs, offs2):
    idx = unstriped(offs)
    idx2 = unstriped(offs2)
    xtu = unpack_weight(xt_words, xt_scales, "e4m3")
    wcu = unpack_weight(wc_words, wc_scales, "e2m1")
    wou = unpack_weight(wo_words, wo_scales, "e4m3")
    sku = unpack_weight(sk_words, sk_scales, "e2m1")
    wsu = unpack_weight(ws_words, ws_scales, "e4m3")
    z = xtu.T @ wcu
    zj = z[:, idx]
    zt = zj.T
    u = zt[:, idx2] * f64(fj)
    uq = mxq(u, 0, "e4m3")
    y = wou.T @ uq + wsu.T @ sku
    return y

@@ -1,0 +1,246 @@
+from contextlib import ExitStack
+
+import concourse.mybir as mybir
+from concourse.masks import make_identity
+
+F32 = mybir.dt.float32
+BF16 = mybir.dt.bfloat16
+I32 = mybir.dt.int32
+U32 = mybir.dt.uint32
+U16 = mybir.dt.uint16
+U8 = mybir.dt.uint8
+FP8X4 = mybir.dt.float8_e4m3fn_x4
+FP4X4 = mybir.dt.float4_e2m1fn_x4
+COPY = mybir.ActivationFunctionType.Copy
+MULT = mybir.AluOpType.mult
+
+FLOPS = 1879048192
+
+P = 128
+T, C, J, I, N = 1024, 1024, 1024, 512, 512
+PASS = 512
+BANK = 512
+CHUNKS = ((0, 256), (256, 128), (384, 128))
+
+
+def tile_list_rows_then_columns_kernel(
+    tc, xt_words, xt_scales, wc_words, wc_scales, fj, wo_words, wo_scales,
+    sk_words, sk_scales, ws_words, ws_scales, offs, offs2, out,
+):
+    nc = tc.nc
+    with ExitStack() as ctx:
+        keep = ctx.enter_context(tc.tile_pool(name="keep", bufs=1))
+        psum = ctx.enter_context(tc.psum_pool(name="psum", bufs=1))
+        banks = [psum.tile([P, BANK], F32, name=f"bank{b}") for b in range(8)]
+
+        def plane(name, width, engine):
+            tile = keep.tile([P, width], U8, name=name, align_bytes=64)
+            engine.memset(tile[:].bitcast(I32), 0)
+            return tile
+
+        def load_scale_rows(tile, rows, queues):
+            for q in range(4):
+                queues[q].dma_start(tile[32 * q : 32 * q + 4, :].bitcast(I32), rows[4 * q : 4 * q + 4, :].bitcast(I32))
+
+        def load_filled_plane(tile, rows, queue, quads):
+            for q in quads:
+                quad = rows[4 * q : 4 * q + 4, :].bitcast(I32)
+                queue.dma_start(
+                    tile[32 * q : 32 * q + 32, :].bitcast(I32), quad.unsqueeze(0).to_broadcast([8, 4, quad.shape[1]])
+                )
+
+        wc_s = keep.tile([P, C], U8, name="wc_s", align_bytes=64)
+        xt_s = keep.tile([P, T], U8, name="xt_s", align_bytes=64)
+
+        wc_w = keep.tile([P, 2 * C], U8, name="wc_w", align_bytes=64)
+        xt_flat = xt_words[0].rearrange("p t r -> p (t r)").bitcast(I32)
+        xt_parts = ((0, 1), (1, 4), (4, 8))
+        xt_w = {}
+
+        def load_tokens(first, last):
+            tile = keep.tile([P, (last - first) * P], U32, name=f"xt_w{first}", align_bytes=64)
+            nc.sync.dma_start(tile[:].bitcast(I32), xt_flat[:, first * P : last * P])
+            for t in range(first, last):
+                xt_w[t] = tile[:, (t - first) * P : (t - first + 1) * P]
+
+        load_filled_plane(wc_s, wc_scales[0], nc.sync, (0,))
+        load_filled_plane(xt_s, xt_scales[0], nc.scalar, range(4))
+        nc.sync.dma_start(wc_w[:].bitcast(I32), wc_words[0].bitcast(I32))
+        load_tokens(*xt_parts[0])
+        load_filled_plane(wc_s, wc_scales[0], nc.sync, (1, 2, 3))
+        idx = keep.tile([P, J // 16], U16, name="idx")
+        nc.sync.dma_start(idx[:], offs)
+        load_tokens(*xt_parts[1])
+        load_tokens(*xt_parts[2])
+        idx2 = keep.tile([P, I // 16], U16, name="idx2")
+        nc.sync.dma_start(idx2[:], offs2)
+
+        ident = keep.tile([P, P], F32, name="ident")
+        nc.vector.memset(ident[:], 0.0)
+        make_identity(nc, ident[:], nomemset=True)
+
+        wo_s = plane("wo_s", 2 * N, nc.vector)
+        ws_s = plane("ws_s", N, nc.vector)
+        sk_s = plane("sk_s", I, nc.vector)
+        factor = keep.tile([P, 2, 4], F32, name="factor")
+        nc.sync.dma_start(factor[:], fj.rearrange("(a p s) o -> p a (s o)", a=2, s=4))
+        wo_w = keep.tile([P, 2, N], U32, name="wo_w", align_bytes=64)
+        nc.sync.dma_start(wo_w[:].bitcast(I32), wo_words.rearrange("a p n r -> p a (n r)").bitcast(I32))
+        ws_w = keep.tile([P, N], U32, name="ws_w", align_bytes=64)
+        nc.sync.dma_start(ws_w[:].bitcast(I32), ws_words[0].rearrange("p n r -> p (n r)").bitcast(I32))
+        sk_w = keep.tile([P, 2 * I], U8, name="sk_w", align_bytes=64)
+        nc.sync.dma_start(sk_w[:].bitcast(I32), sk_words[0].bitcast(I32))
+        for q in range(4):
+            nc.sync.dma_start(
+                wo_s[32 * q : 32 * q + 4, :].bitcast(I32).rearrange("r (a n) -> r a n", a=2),
+                wo_scales[:, 4 * q : 4 * q + 4, :].bitcast(I32).rearrange("a r n -> r a n"),
+            )
+        load_scale_rows(ws_s, ws_scales[0], [nc.sync] * 4)
+        load_scale_rows(sk_s, sk_scales[0], [nc.sync] * 4)
+
+        z = []
+        for t in range(T // P):
+            z_t = keep.tile([P, C], F32, name=f"z{t}")
+            z.append(z_t)
+            for h in range(2):
+                bank = banks[2 * (t % 2) + h]
+                cols = slice(h * BANK, (h + 1) * BANK)
+                nc.tensor.matmul_mx(
+                    bank[:], lhsT=xt_w[t].bitcast(FP8X4), lhsT_scale=xt_s[:, t * P : (t + 1) * P],
+                    rhs=wc_w[:, 2 * h * BANK : 2 * (h + 1) * BANK].bitcast(FP4X4), rhs_scale=wc_s[:, cols],
+                    start=True, stop=True,
+                )
+                if t == 0 and h == 0:
+                    nc.scalar.activation(z_t[:, cols], bank[:], COPY)
+                elif t == 0:
+                    nc.vector.tensor_copy(z_t[:, cols], bank[:])
+                else:
+                    nc.scalar.copy(z_t[:, cols], bank[:])
+
+        zt = [keep.tile([P, 4, T], F32, name=f"zt{a}") for a in range(2)]
+        for t in range(T // P):
+            for a in range(2):
+                zj = keep.tile([P, PASS], F32, name=f"zj{t}_{a}")
+                nc.vector.tensor_copy(
+                    zj[:].bitcast(U32).rearrange("p (s q) -> p q s", s=4),
+                    z[t][:].bitcast(U32).indirect(idx[:, 32 * a : 32 * (a + 1)]),
+                )
+                bank = banks[4 + (2 * t + a) % 4]
+                for s in range(4):
+                    nc.tensor.transpose(bank[:, s * P : (s + 1) * P], zj[:, s * P : (s + 1) * P], ident[:])
+                nc.scalar.copy(zt[a][:, :, t * P : (t + 1) * P], bank[:].rearrange("p (s t) -> p s t", s=4))
+
+        codes, scales, woven = {}, {}, {}
+
+        def pick(c, a, picked):
+            first, width = CHUNKS[c]
+            for s in range(4):
+                nc.vector.tensor_copy(
+                    picked[:, s, :], zt[a][:, s, :].indirect(idx2[:, first // 16 : (first + width) // 16])
+                )
+
+        def scale_and_weave(c, a, picked, tag):
+            width = CHUNKS[c][1]
+            rows = keep.tile([P, 4, width], BF16, name=f"rows{c}_{a}")
+            for s in range(4):
+                nc.scalar.activation(rows[:, s, :], picked[:, s, :], COPY, scale=factor[:, a, s : s + 1])
+            woven[c, a] = keep.tile([P, width, 4], BF16, name=f"woven{c}_{a}", tag=tag, align_bytes=64)
+            nc.scalar.copy(
+                woven[c, a][:].rearrange("p (g i) s -> p g s i", i=4),
+                rows[:].rearrange("p s (g i) -> p g s i", i=4),
+            )
+
+        def quantise(c, a):
+            width = CHUNKS[c][1]
+            codes[c, a] = keep.tile([P, width], U32, name=f"codes{c}_{a}", align_bytes=64)
+            scales[c, a] = keep.tile([P, width], U8, name=f"scales{c}_{a}", align_bytes=64)
+            nc.vector.quantize_mx(
+                codes[c, a][:].bitcast(FP8X4), scales[c, a][:], woven[c, a][:].rearrange("p i s -> p (i s)")
+            )
+
+        def place(c, m):
+            width = CHUNKS[c][1]
+            if c == 2:
+                return banks[4 + m][:, :width]
+            return banks[2 * c + m % 2][:, (m // 2) * width : (m // 2 + 1) * width]
+
+        def skip_pass(c, m):
+            first, width = CHUNKS[c]
+            for i0 in range(0, width, P):
+                nc.tensor.matmul_mx(
+                    place(c, m)[:, i0 : i0 + P], lhsT=ws_w[:, m * P : (m + 1) * P].bitcast(FP8X4),
+                    lhsT_scale=ws_s[:, m * P : (m + 1) * P],
+                    rhs=sk_w[:, 2 * (first + i0) : 2 * (first + i0 + P)].bitcast(FP4X4),
+                    rhs_scale=sk_s[:, first + i0 : first + i0 + P], start=(i0 == 0), stop=False,
+                )
+
+        def u_pass(c, m, a):
+            nc.tensor.matmul_mx(
+                place(c, m), lhsT=wo_w[:, a, m * P : (m + 1) * P].bitcast(FP8X4),
+                lhsT_scale=wo_s[:, a * N + m * P : a * N + (m + 1) * P],
+                rhs=codes[c, a][:].bitcast(FP8X4), rhs_scale=scales[c, a][:], start=False, stop=(a == 1),
+            )
+
+        out_v = out.rearrange("(m p) i -> p m i", p=P)
+
+        def open_groups(c, ms):
+            for m in ms:
+                skip_pass(c, m)
+            for m in ms:
+                u_pass(c, m, 0)
+
+        def finish_paired(c):
+            first, width = CHUNKS[c]
+            for m in (0, 1):
+                u_pass(c, m, 1)
+            open_groups(c, (2, 3))
+            for m in (2, 3):
+                u_pass(c, m, 1)
+            result = keep.tile([P, 4, width], F32, name=f"result{c}")
+            for b in range(2):
+                nc.scalar.copy(
+                    result[:, b::2, :], banks[2 * c + b][:, : 2 * width].rearrange("p (m i) -> p m i", m=2)
+                )
+            nc.sync.dma_start(out_v[:, :, first : first + width], result[:])
+
+        picked00 = keep.tile([P, 4, 256], F32, name="picked00")
+        picked01 = keep.tile([P, 4, 256], F32, name="picked01")
+        pick(0, 0, picked00)
+        scale_and_weave(0, 0, picked00, "turn_a")
+        pick(0, 1, picked01)
+        scale_and_weave(0, 1, picked01, "turn_b")
+        quantise(0, 0)
+        open_groups(0, (0, 1))
+        picked1 = keep.tile([P, 2, 4, 128], F32, name="picked1", tag="turn_a", align_bytes=64)
+        pick(1, 0, picked1[:, 0])
+        scale_and_weave(1, 0, picked1[:, 0], "turn_c")
+        pick(1, 1, picked1[:, 1])
+        scale_and_weave(1, 1, picked1[:, 1], "turn_d")
+        quantise(0, 1)
+        picked20 = keep.tile([P, 4, 128], F32, name="picked20", tag="turn_b", align_bytes=64)
+        pick(2, 0, picked20)
+        scale_and_weave(2, 0, picked20, "turn_e")
+        quantise(1, 0)
+        open_groups(1, (0, 1))
+        picked21 = keep.tile([P, 4, 128], F32, name="picked21", tag="turn_c", align_bytes=64)
+        pick(2, 1, picked21)
+        quantise(1, 1)
+        finish_paired(0)
+        woven[2, 1] = keep.tile([P, 128, 4], BF16, name="woven2_1", tag="turn_d", align_bytes=64)
+        nc.vector.tensor_tensor(
+            woven[2, 1][:], picked21[:].rearrange("p s i -> p i s"),
+            factor[:, 1, :].unsqueeze(1).to_broadcast([P, 128, 4]), MULT,
+        )
+        quantise(2, 0)
+        finish_paired(1)
+        open_groups(2, range(4))
+        quantise(2, 1)
+        first, width = CHUNKS[2]
+        result = keep.tile([P, 4, width], F32, name="result2")
+        for m in range(4):
+            u_pass(2, m, 1)
+            if m % 2 == 0:
+                nc.scalar.copy(result[:, m, :], place(2, m))
+            else:
+                nc.vector.tensor_copy(result[:, m, :], place(2, m))
+        nc.sync.dma_start(out_v[:, :, first : first + width], result[:])

@@ -30,6 +30,7 @@ def tile_list_rows_then_columns_kernel(
     nc = tc.nc
     with ExitStack() as ctx:
         keep = ctx.enter_context(tc.tile_pool(name="keep", bufs=1))
+        turns = ctx.enter_context(tc.tile_pool(name="turns", bufs=1))
         psum = ctx.enter_context(tc.psum_pool(name="psum", bufs=1))
         banks = [psum.tile([P, BANK], F32, name=f"bank{b}") for b in range(8)]
 
@@ -98,149 +99,161 @@ def tile_list_rows_then_columns_kernel(
         load_scale_rows(ws_s, ws_scales[0], [nc.sync] * 4)
         load_scale_rows(sk_s, sk_scales[0], [nc.sync] * 4)
 
-        z = []
-        for t in range(T // P):
-            z_t = keep.tile([P, C], F32, name=f"z{t}")
-            z.append(z_t)
+        def z_pass(t, bank, first, width):
+            nc.tensor.matmul_mx(
+                bank[:, :width], lhsT=xt_w[t].bitcast(FP8X4), lhsT_scale=xt_s[:, t * P : (t + 1) * P],
+                rhs=wc_w[:, 2 * first : 2 * (first + width)].bitcast(FP4X4), rhs_scale=wc_s[:, first : first + width],
+                start=True, stop=True,
+            )
+
+        z, window = {}, {}
+        for t in range(6):
+            z[t] = window[t] = keep.tile([P, C], F32, name=f"z{t}")[:]
+        last_two = keep.tile([P, 2 * C], F32, name="z_last_two")
+        z[6], z[7] = last_two[:, :C], last_two[:, C:]
+        window[6], window[7] = last_two[:], z[7]
+        for quarter in range(4):
+            first = quarter * 256
+            bank = banks[4 + quarter]
+            z_pass(0, bank, first, 256)
+            if quarter % 2 == 0:
+                nc.scalar.activation(z[0][:, first : first + 256], bank[:, :256], COPY)
+            else:
+                nc.vector.tensor_copy(z[0][:, first : first + 256], bank[:, :256])
+        for t in range(1, T // P):
             for h in range(2):
-                bank = banks[2 * (t % 2) + h]
-                cols = slice(h * BANK, (h + 1) * BANK)
-                nc.tensor.matmul_mx(
-                    bank[:], lhsT=xt_w[t].bitcast(FP8X4), lhsT_scale=xt_s[:, t * P : (t + 1) * P],
-                    rhs=wc_w[:, 2 * h * BANK : 2 * (h + 1) * BANK].bitcast(FP4X4), rhs_scale=wc_s[:, cols],
-                    start=True, stop=True,
-                )
-                if t == 0 and h == 0:
-                    nc.scalar.activation(z_t[:, cols], bank[:], COPY)
-                elif t == 0:
-                    nc.vector.tensor_copy(z_t[:, cols], bank[:])
-                else:
-                    nc.scalar.copy(z_t[:, cols], bank[:])
+                bank = banks[2 * ((t - 1) % 2) + h]
+                z_pass(t, bank, h * BANK, BANK)
+                nc.scalar.copy(z[t][:, h * BANK : (h + 1) * BANK], bank[:])
 
         zt = [keep.tile([P, 4, T], F32, name=f"zt{a}") for a in range(2)]
-        for t in range(T // P):
-            for a in range(2):
-                zj = keep.tile([P, PASS], F32, name=f"zj{t}_{a}")
-                nc.vector.tensor_copy(
-                    zj[:].bitcast(U32).rearrange("p (s q) -> p q s", s=4),
-                    z[t][:].bitcast(U32).indirect(idx[:, 32 * a : 32 * (a + 1)]),
-                )
-                bank = banks[4 + (2 * t + a) % 4]
-                for s in range(4):
-                    nc.tensor.transpose(bank[:, s * P : (s + 1) * P], zj[:, s * P : (s + 1) * P], ident[:])
-                nc.scalar.copy(zt[a][:, :, t * P : (t + 1) * P], bank[:].rearrange("p (s t) -> p s t", s=4))
+        steps = [(t, a) for t in range(6) for a in range(2)] + [(t, a) for a in range(2) for t in (6, 7)]
+        for step, (t, a) in enumerate(steps):
+            zj = keep.tile([P, PASS], F32, name=f"zj{t}_{a}")
+            nc.vector.tensor_copy(
+                zj[:].bitcast(U32).rearrange("p (s q) -> p q s", s=4),
+                window[t].bitcast(U32).indirect(idx[:, 32 * a : 32 * (a + 1)]),
+            )
+            bank = banks[4 + step % 4]
+            for s in range(4):
+                nc.tensor.transpose(bank[:, s * P : (s + 1) * P], zj[:, s * P : (s + 1) * P], ident[:])
+            nc.scalar.copy(zt[a][:, :, t * P : (t + 1) * P], bank[:].rearrange("p (s t) -> p s t", s=4))
 
-        codes, scales, woven = {}, {}, {}
+        codes, scales = {}, {}
 
-        def pick(c, a, picked):
-            first, width = CHUNKS[c]
+        def pick(a, first, width, picked):
             for s in range(4):
                 nc.vector.tensor_copy(
-                    picked[:, s, :], zt[a][:, s, :].indirect(idx2[:, first // 16 : (first + width) // 16])
+                    picked[:, s * width : (s + 1) * width],
+                    zt[a][:, s, :].indirect(idx2[:, first // 16 : (first + width) // 16]),
                 )
 
-        def scale_and_weave(c, a, picked, tag):
-            width = CHUNKS[c][1]
-            rows = keep.tile([P, 4, width], BF16, name=f"rows{c}_{a}")
+        def scale_and_weave(a, width, picked, rows, woven):
             for s in range(4):
-                nc.scalar.activation(rows[:, s, :], picked[:, s, :], COPY, scale=factor[:, a, s : s + 1])
-            woven[c, a] = keep.tile([P, width, 4], BF16, name=f"woven{c}_{a}", tag=tag, align_bytes=64)
+                cols = slice(s * width, (s + 1) * width)
+                nc.scalar.activation(rows[:, cols], picked[:, cols], COPY, scale=factor[:, a, s : s + 1])
             nc.scalar.copy(
-                woven[c, a][:].rearrange("p (g i) s -> p g s i", i=4),
-                rows[:].rearrange("p s (g i) -> p g s i", i=4),
+                woven.rearrange("p (g i s) -> p g s i", i=4, s=4),
+                rows.rearrange("p (s g i) -> p g s i", s=4, i=4),
             )
 
-        def quantise(c, a):
-            width = CHUNKS[c][1]
-            codes[c, a] = keep.tile([P, width], U32, name=f"codes{c}_{a}", align_bytes=64)
-            scales[c, a] = keep.tile([P, width], U8, name=f"scales{c}_{a}", align_bytes=64)
-            nc.vector.quantize_mx(
-                codes[c, a][:].bitcast(FP8X4), scales[c, a][:], woven[c, a][:].rearrange("p i s -> p (i s)")
-            )
+        def quantise(a, first, width, woven):
+            words = keep.tile([P, width], U32, name=f"codes{a}_{first}", align_bytes=64)
+            plane_u = keep.tile([P, width], U8, name=f"scales{a}_{first}", align_bytes=64)
+            nc.vector.quantize_mx(words[:].bitcast(FP8X4), plane_u[:], woven)
+            for c, (c_first, c_width) in enumerate(CHUNKS):
+                if first <= c_first < first + width:
+                    cols = slice(c_first - first, c_first - first + c_width)
+                    codes[c, a], scales[c, a] = words[:, cols], plane_u[:, cols]
 
         def place(c, m):
             width = CHUNKS[c][1]
             if c == 2:
                 return banks[4 + m][:, :width]
-            return banks[2 * c + m % 2][:, (m // 2) * width : (m // 2 + 1) * width]
+            return banks[2 * c + m // 2][:, (m % 2) * width : (m % 2 + 1) * width]
 
-        def skip_pass(c, m):
+        def skip_passes(c):
             first, width = CHUNKS[c]
-            for i0 in range(0, width, P):
-                nc.tensor.matmul_mx(
-                    place(c, m)[:, i0 : i0 + P], lhsT=ws_w[:, m * P : (m + 1) * P].bitcast(FP8X4),
-                    lhsT_scale=ws_s[:, m * P : (m + 1) * P],
-                    rhs=sk_w[:, 2 * (first + i0) : 2 * (first + i0 + P)].bitcast(FP4X4),
-                    rhs_scale=sk_s[:, first + i0 : first + i0 + P], start=(i0 == 0), stop=False,
-                )
+            for m in range(4):
+                for i0 in range(0, width, P):
+                    nc.tensor.matmul_mx(
+                        place(c, m)[:, i0 : i0 + P], lhsT=ws_w[:, m * P : (m + 1) * P].bitcast(FP8X4),
+                        lhsT_scale=ws_s[:, m * P : (m + 1) * P],
+                        rhs=sk_w[:, 2 * (first + i0) : 2 * (first + i0 + P)].bitcast(FP4X4),
+                        rhs_scale=sk_s[:, first + i0 : first + i0 + P],
+                        start=(i0 == 0 and (c == 2 or m % 2 == 0)), stop=False,
+                    )
 
         def u_pass(c, m, a):
             nc.tensor.matmul_mx(
                 place(c, m), lhsT=wo_w[:, a, m * P : (m + 1) * P].bitcast(FP8X4),
                 lhsT_scale=wo_s[:, a * N + m * P : a * N + (m + 1) * P],
-                rhs=codes[c, a][:].bitcast(FP8X4), rhs_scale=scales[c, a][:], start=False, stop=(a == 1),
+                rhs=codes[c, a].bitcast(FP8X4), rhs_scale=scales[c, a],
+                start=False, stop=(a == 1 and (c == 2 or m % 2 == 1)),
             )
 
         out_v = out.rearrange("(m p) i -> p m i", p=P)
 
-        def open_groups(c, ms):
-            for m in ms:
-                skip_pass(c, m)
-            for m in ms:
+        def finish_paired(c, result):
+            first, width = CHUNKS[c]
+            for m in range(4):
+                u_pass(c, m, 1)
+            for b in range(2):
+                half = result[:, 2 * b * width : 2 * (b + 1) * width]
+                nc.scalar.copy(half, banks[2 * c + b][:, : 2 * width])
+                nc.sync.dma_start(
+                    out_v[:, 2 * b : 2 * b + 2, first : first + width], half.rearrange("p (m i) -> p m i", m=2)
+                )
+
+        def own(name, dtype, width):
+            return keep.tile([P, width], dtype, name=name, align_bytes=64)[:]
+
+        def shared(name, dtype, width, offset):
+            return turns.tile([P, width], dtype, name=name, align_bytes=64, offset=offset)[:]
+
+        for c in range(3):
+            skip_passes(c)
+
+        picked_a, woven_a = own("picked_a", F32, 1024), own("woven_a", BF16, 1024)
+        pick(0, 0, 256, picked_a)
+        scale_and_weave(0, 256, picked_a, shared("rows_a", BF16, 1024, 4096), woven_a)
+        picked_b, woven_b = own("picked_b", F32, 1024), own("woven_b", BF16, 1024)
+        pick(1, 0, 256, picked_b)
+        scale_and_weave(1, 256, picked_b, shared("rows_b", BF16, 1024, 5120), woven_b)
+        quantise(0, 0, 256, woven_a)
+        for m in range(4):
+            u_pass(0, m, 0)
+
+        picked_c, woven_c = shared("picked_c", F32, 1024, 256), own("woven_c", BF16, 1024)
+        pick(0, 256, 256, picked_c)
+        scale_and_weave(0, 256, picked_c, shared("rows_c", BF16, 1024, 6400), woven_c)
+        quantise(1, 0, 256, woven_b)
+
+        picked_d, woven_d = shared("picked_d", F32, 512, 4352), own("woven_d", BF16, 512)
+        pick(1, 256, 128, picked_d)
+        scale_and_weave(1, 128, picked_d, shared("rows_d", BF16, 512, 6400), woven_d)
+        quantise(0, 256, 256, woven_c)
+        finish_paired(0, shared("result0", F32, 1024, 2816))
+        for c in (1, 2):
+            for m in range(4):
                 u_pass(c, m, 0)
 
-        def finish_paired(c):
-            first, width = CHUNKS[c]
-            for m in (0, 1):
-                u_pass(c, m, 1)
-            open_groups(c, (2, 3))
-            for m in (2, 3):
-                u_pass(c, m, 1)
-            result = keep.tile([P, 4, width], F32, name=f"result{c}")
-            for b in range(2):
-                nc.scalar.copy(
-                    result[:, b::2, :], banks[2 * c + b][:, : 2 * width].rearrange("p (m i) -> p m i", m=2)
-                )
-            nc.sync.dma_start(out_v[:, :, first : first + width], result[:])
-
-        picked00 = keep.tile([P, 4, 256], F32, name="picked00")
-        picked01 = keep.tile([P, 4, 256], F32, name="picked01")
-        pick(0, 0, picked00)
-        scale_and_weave(0, 0, picked00, "turn_a")
-        pick(0, 1, picked01)
-        scale_and_weave(0, 1, picked01, "turn_b")
-        quantise(0, 0)
-        open_groups(0, (0, 1))
-        picked1 = keep.tile([P, 2, 4, 128], F32, name="picked1", tag="turn_a", align_bytes=64)
-        pick(1, 0, picked1[:, 0])
-        scale_and_weave(1, 0, picked1[:, 0], "turn_c")
-        pick(1, 1, picked1[:, 1])
-        scale_and_weave(1, 1, picked1[:, 1], "turn_d")
-        quantise(0, 1)
-        picked20 = keep.tile([P, 4, 128], F32, name="picked20", tag="turn_b", align_bytes=64)
-        pick(2, 0, picked20)
-        scale_and_weave(2, 0, picked20, "turn_e")
-        quantise(1, 0)
-        open_groups(1, (0, 1))
-        picked21 = keep.tile([P, 4, 128], F32, name="picked21", tag="turn_c", align_bytes=64)
-        pick(2, 1, picked21)
-        quantise(1, 1)
-        finish_paired(0)
-        woven[2, 1] = keep.tile([P, 128, 4], BF16, name="woven2_1", tag="turn_d", align_bytes=64)
+        picked_e = shared("picked_e", F32, 512, 7936)
+        pick(1, 384, 128, picked_e)
+        quantise(1, 256, 128, woven_d)
+        finish_paired(1, own("result1", F32, 512))
+        woven_e = shared("woven_e", BF16, 512, 6912)
         nc.vector.tensor_tensor(
-            woven[2, 1][:], picked21[:].rearrange("p s i -> p i s"),
-            factor[:, 1, :].unsqueeze(1).to_broadcast([P, 128, 4]), MULT,
+            woven_e.rearrange("p (g i s) -> p g s i", i=2, s=4), picked_e.rearrange("p (s g i) -> p g s i", s=4, i=2),
+            factor[:, 1, :].unsqueeze(1).unsqueeze(3).to_broadcast([P, 64, 4, 2]), MULT,
         )
-        quantise(2, 0)
-        finish_paired(1)
-        open_groups(2, range(4))
-        quantise(2, 1)
+        quantise(1, 384, 128, woven_e)
         first, width = CHUNKS[2]
-        result = keep.tile([P, 4, width], F32, name="result2")
-        for m in range(4):
-            u_pass(2, m, 1)
-            if m % 2 == 0:
-                nc.scalar.copy(result[:, m, :], place(2, m))
-            else:
-                nc.vector.tensor_copy(result[:, m, :], place(2, m))
-        nc.sync.dma_start(out_v[:, :, first : first + width], result[:])
+        for pair in range(2):
+            result = keep.tile([P, 2, width], F32, name=f"result2_{pair}")
+            for m in (2 * pair, 2 * pair + 1):
+                u_pass(2, m, 1)
+            nc.scalar.copy(result[:, 0, :], place(2, 2 * pair))
+            nc.vector.tensor_copy(result[:, 1, :], place(2, 2 * pair + 1))
+            queue = nc.sync if pair == 0 else nc.scalar
+            queue.dma_start(out_v[:, 2 * pair : 2 * pair + 2, first : first + width], result[:])

@@ -106,38 +106,37 @@ def tile_list_rows_then_columns_kernel(
                 start=True, stop=True,
             )
 
-        z, window = {}, {}
-        for t in range(6):
-            z[t] = window[t] = keep.tile([P, C], F32, name=f"z{t}")[:]
-        last_two = keep.tile([P, 2 * C], F32, name="z_last_two")
-        z[6], z[7] = last_two[:, :C], last_two[:, C:]
-        window[6], window[7] = last_two[:], z[7]
+        z = keep.tile([P, (T // P) * C], F32, name="z")
         for quarter in range(4):
             first = quarter * 256
             bank = banks[4 + quarter]
             z_pass(0, bank, first, 256)
             if quarter % 2 == 0:
-                nc.scalar.activation(z[0][:, first : first + 256], bank[:, :256], COPY)
+                nc.scalar.activation(z[:, first : first + 256], bank[:, :256], COPY)
             else:
-                nc.vector.tensor_copy(z[0][:, first : first + 256], bank[:, :256])
+                nc.vector.tensor_copy(z[:, first : first + 256], bank[:, :256])
         for t in range(1, T // P):
             for h in range(2):
-                bank = banks[2 * ((t - 1) % 2) + h]
+                bank = banks[(2 * (t - 1) + h) % 8]
                 z_pass(t, bank, h * BANK, BANK)
-                nc.scalar.copy(z[t][:, h * BANK : (h + 1) * BANK], bank[:])
+                nc.scalar.copy(z[:, t * C + h * BANK : t * C + (h + 1) * BANK], bank[:])
 
         zt = [keep.tile([P, 4, T], F32, name=f"zt{a}") for a in range(2)]
-        steps = [(t, a) for t in range(6) for a in range(2)] + [(t, a) for a in range(2) for t in (6, 7)]
-        for step, (t, a) in enumerate(steps):
-            zj = keep.tile([P, PASS], F32, name=f"zj{t}_{a}")
+        steps = [(0, (0,), 1), (0, (1,), 1)] + [(t, (0, 1), 2) for t in range(1, 6)]
+        steps = steps + [(6, (0,), 2), (7, (0,), 1), (6, (1,), 2), (7, (1,), 1)]
+        turn = 6
+        for t, passes, span in steps:
+            zj = keep.tile([P, len(passes), PASS], F32, name=f"zj{t}_{passes[0]}")
             nc.vector.tensor_copy(
-                zj[:].bitcast(U32).rearrange("p (s q) -> p q s", s=4),
-                window[t].bitcast(U32).indirect(idx[:, 32 * a : 32 * (a + 1)]),
+                zj[:].bitcast(U32).rearrange("p a (s q) -> p a q s", s=4),
+                z[:, t * C : (t + span) * C].bitcast(U32).indirect(idx[:, 32 * passes[0] : 32 * (passes[-1] + 1)]),
             )
-            bank = banks[4 + step % 4]
-            for s in range(4):
-                nc.tensor.transpose(bank[:, s * P : (s + 1) * P], zj[:, s * P : (s + 1) * P], ident[:])
-            nc.scalar.copy(zt[a][:, :, t * P : (t + 1) * P], bank[:].rearrange("p (s t) -> p s t", s=4))
+            for n, a in enumerate(passes):
+                bank = banks[turn % 8]
+                turn = turn + 1
+                for s in range(4):
+                    nc.tensor.transpose(bank[:, s * P : (s + 1) * P], zj[:, n, s * P : (s + 1) * P], ident[:])
+                nc.scalar.copy(zt[a][:, :, t * P : (t + 1) * P], bank[:].rearrange("p (s t) -> p s t", s=4))
 
         codes, scales = {}, {}
 

@@ -64,11 +64,12 @@ def tile_list_rows_then_columns_kernel(
             for t in range(first, last):
                 xt_w[t] = tile[:, (t - first) * P : (t - first + 1) * P]
 
-        load_filled_plane(wc_s, wc_scales[0], nc.sync, (0,))
-        load_filled_plane(xt_s, xt_scales[0], nc.scalar, range(4))
+        wc_rows = wc_scales[0].bitcast(I32)
+        nc.scalar.dma_start(wc_s[:98, :].bitcast(I32), wc_rows[:14, :].unsqueeze(0).to_broadcast([7, 14, C // 4]))
         nc.sync.dma_start(wc_w[:].bitcast(I32), wc_words[0].bitcast(I32))
         load_tokens(*xt_parts[0])
-        load_filled_plane(wc_s, wc_scales[0], nc.sync, (1, 2, 3))
+        load_filled_plane(xt_s, xt_scales[0], nc.sync, range(4))
+        nc.sync.dma_start(wc_s[98:, :].bitcast(I32), wc_rows[14:, :].unsqueeze(0).to_broadcast([15, 2, C // 4]))
         idx = keep.tile([P, J // 16], U16, name="idx")
         nc.sync.dma_start(idx[:], offs)
         load_tokens(*xt_parts[1])

from contextlib import ExitStack

import concourse.mybir as mybir
from concourse.masks import make_identity

F32 = mybir.dt.float32
BF16 = mybir.dt.bfloat16
I32 = mybir.dt.int32
U32 = mybir.dt.uint32
U16 = mybir.dt.uint16
U8 = mybir.dt.uint8
FP8X4 = mybir.dt.float8_e4m3fn_x4
FP4X4 = mybir.dt.float4_e2m1fn_x4
COPY = mybir.ActivationFunctionType.Copy
MULT = mybir.AluOpType.mult

FLOPS = 1879048192

P = 128
T, C, J, I, N = 1024, 1024, 1024, 512, 512
PASS = 512
BANK = 512
CHUNKS = ((0, 256), (256, 128), (384, 128))


def tile_list_rows_then_columns_kernel(
    tc, xt_words, xt_scales, wc_words, wc_scales, fj, wo_words, wo_scales,
    sk_words, sk_scales, ws_words, ws_scales, offs, offs2, out,
):
    nc = tc.nc
    with ExitStack() as ctx:
        keep = ctx.enter_context(tc.tile_pool(name="keep", bufs=1))
        turns = ctx.enter_context(tc.tile_pool(name="turns", bufs=1))
        psum = ctx.enter_context(tc.psum_pool(name="psum", bufs=1))
        banks = [psum.tile([P, BANK], F32, name=f"bank{b}") for b in range(8)]

        def plane(name, width, engine):
            tile = keep.tile([P, width], U8, name=name, align_bytes=64)
            engine.memset(tile[:].bitcast(I32), 0)
            return tile

        def load_scale_rows(tile, rows, queues):
            for q in range(4):
                queues[q].dma_start(tile[32 * q : 32 * q + 4, :].bitcast(I32), rows[4 * q : 4 * q + 4, :].bitcast(I32))

        def load_filled_plane(tile, rows, queue, quads):
            for q in quads:
                quad = rows[4 * q : 4 * q + 4, :].bitcast(I32)
                queue.dma_start(
                    tile[32 * q : 32 * q + 32, :].bitcast(I32), quad.unsqueeze(0).to_broadcast([8, 4, quad.shape[1]])
                )

        wc_s = keep.tile([P, C], U8, name="wc_s", align_bytes=64)
        xt_s = keep.tile([P, T], U8, name="xt_s", align_bytes=64)

        wc_w = keep.tile([P, 2 * C], U8, name="wc_w", align_bytes=64)
        xt_flat = xt_words[0].rearrange("p t r -> p (t r)").bitcast(I32)
        xt_parts = ((0, 1), (1, 4), (4, 8))
        xt_w = {}

        def load_tokens(first, last):
            tile = keep.tile([P, (last - first) * P], U32, name=f"xt_w{first}", align_bytes=64)
            nc.sync.dma_start(tile[:].bitcast(I32), xt_flat[:, first * P : last * P])
            for t in range(first, last):
                xt_w[t] = tile[:, (t - first) * P : (t - first + 1) * P]

        wc_rows = wc_scales[0].bitcast(I32)
        nc.scalar.dma_start(wc_s[:98, :].bitcast(I32), wc_rows[:14, :].unsqueeze(0).to_broadcast([7, 14, C // 4]))
        nc.sync.dma_start(wc_w[:].bitcast(I32), wc_words[0].bitcast(I32))
        load_tokens(*xt_parts[0])
        load_filled_plane(xt_s, xt_scales[0], nc.sync, range(4))
        nc.sync.dma_start(wc_s[98:, :].bitcast(I32), wc_rows[14:, :].unsqueeze(0).to_broadcast([15, 2, C // 4]))
        idx = keep.tile([P, J // 16], U16, name="idx")
        nc.sync.dma_start(idx[:], offs)
        load_tokens(*xt_parts[1])
        load_tokens(*xt_parts[2])
        idx2 = keep.tile([P, I // 16], U16, name="idx2")
        nc.sync.dma_start(idx2[:], offs2)

        ident = keep.tile([P, P], F32, name="ident")
        nc.vector.memset(ident[:], 0.0)
        make_identity(nc, ident[:], nomemset=True)

        wo_s = plane("wo_s", 2 * N, nc.vector)
        ws_s = plane("ws_s", N, nc.vector)
        sk_s = plane("sk_s", I, nc.vector)
        factor = keep.tile([P, 2, 4], F32, name="factor")
        nc.sync.dma_start(factor[:], fj.rearrange("(a p s) o -> p a (s o)", a=2, s=4))
        wo_w = keep.tile([P, 2, N], U32, name="wo_w", align_bytes=64)
        nc.sync.dma_start(wo_w[:].bitcast(I32), wo_words.rearrange("a p n r -> p a (n r)").bitcast(I32))
        ws_w = keep.tile([P, N], U32, name="ws_w", align_bytes=64)
        nc.sync.dma_start(ws_w[:].bitcast(I32), ws_words[0].rearrange("p n r -> p (n r)").bitcast(I32))
        sk_w = keep.tile([P, 2 * I], U8, name="sk_w", align_bytes=64)
        nc.sync.dma_start(sk_w[:].bitcast(I32), sk_words[0].bitcast(I32))
        for q in range(4):
            nc.sync.dma_start(
                wo_s[32 * q : 32 * q + 4, :].bitcast(I32).rearrange("r (a n) -> r a n", a=2),
                wo_scales[:, 4 * q : 4 * q + 4, :].bitcast(I32).rearrange("a r n -> r a n"),
            )
        load_scale_rows(ws_s, ws_scales[0], [nc.sync] * 4)
        load_scale_rows(sk_s, sk_scales[0], [nc.sync] * 4)

        def z_pass(t, bank, first, width):
            nc.tensor.matmul_mx(
                bank[:, :width], lhsT=xt_w[t].bitcast(FP8X4), lhsT_scale=xt_s[:, t * P : (t + 1) * P],
                rhs=wc_w[:, 2 * first : 2 * (first + width)].bitcast(FP4X4), rhs_scale=wc_s[:, first : first + width],
                start=True, stop=True,
            )

        z = keep.tile([P, (T // P) * C], F32, name="z")
        for quarter in range(4):
            first = quarter * 256
            bank = banks[4 + quarter]
            z_pass(0, bank, first, 256)
            if quarter % 2 == 0:
                nc.scalar.activation(z[:, first : first + 256], bank[:, :256], COPY)
            else:
                nc.vector.tensor_copy(z[:, first : first + 256], bank[:, :256])
        for t in range(1, T // P):
            for h in range(2):
                bank = banks[(2 * (t - 1) + h) % 8]
                z_pass(t, bank, h * BANK, BANK)
                nc.scalar.copy(z[:, t * C + h * BANK : t * C + (h + 1) * BANK], bank[:])

        zt = [keep.tile([P, 4, T], F32, name=f"zt{a}") for a in range(2)]
        steps = [(0, (0,), 1), (0, (1,), 1)] + [(t, (0, 1), 2) for t in range(1, 6)]
        steps = steps + [(6, (0,), 2), (7, (0,), 1), (6, (1,), 2), (7, (1,), 1)]
        turn = 6
        for t, passes, span in steps:
            zj = keep.tile([P, len(passes), PASS], F32, name=f"zj{t}_{passes[0]}")
            nc.vector.tensor_copy(
                zj[:].bitcast(U32).rearrange("p a (s q) -> p a q s", s=4),
                z[:, t * C : (t + span) * C].bitcast(U32).indirect(idx[:, 32 * passes[0] : 32 * (passes[-1] + 1)]),
            )
            for n, a in enumerate(passes):
                bank = banks[turn % 8]
                turn = turn + 1
                for s in range(4):
                    nc.tensor.transpose(bank[:, s * P : (s + 1) * P], zj[:, n, s * P : (s + 1) * P], ident[:])
                nc.scalar.copy(zt[a][:, :, t * P : (t + 1) * P], bank[:].rearrange("p (s t) -> p s t", s=4))

        codes, scales = {}, {}

        def pick(a, first, width, picked):
            for s in range(4):
                nc.vector.tensor_copy(
                    picked[:, s * width : (s + 1) * width],
                    zt[a][:, s, :].indirect(idx2[:, first // 16 : (first + width) // 16]),
                )

        def scale_and_weave(a, width, picked, rows, woven):
            for s in range(4):
                cols = slice(s * width, (s + 1) * width)
                nc.scalar.activation(rows[:, cols], picked[:, cols], COPY, scale=factor[:, a, s : s + 1])
            nc.scalar.copy(
                woven.rearrange("p (g i s) -> p g s i", i=4, s=4),
                rows.rearrange("p (s g i) -> p g s i", s=4, i=4),
            )

        def quantise(a, first, width, woven):
            words = keep.tile([P, width], U32, name=f"codes{a}_{first}", align_bytes=64)
            plane_u = keep.tile([P, width], U8, name=f"scales{a}_{first}", align_bytes=64)
            nc.vector.quantize_mx(words[:].bitcast(FP8X4), plane_u[:], woven)
            for c, (c_first, c_width) in enumerate(CHUNKS):
                if first <= c_first < first + width:
                    cols = slice(c_first - first, c_first - first + c_width)
                    codes[c, a], scales[c, a] = words[:, cols], plane_u[:, cols]

        def place(c, m):
            width = CHUNKS[c][1]
            if c == 2:
                return banks[4 + m][:, :width]
            return banks[2 * c + m // 2][:, (m % 2) * width : (m % 2 + 1) * width]

        def skip_passes(c):
            first, width = CHUNKS[c]
            for m in range(4):
                for i0 in range(0, width, P):
                    nc.tensor.matmul_mx(
                        place(c, m)[:, i0 : i0 + P], lhsT=ws_w[:, m * P : (m + 1) * P].bitcast(FP8X4),
                        lhsT_scale=ws_s[:, m * P : (m + 1) * P],
                        rhs=sk_w[:, 2 * (first + i0) : 2 * (first + i0 + P)].bitcast(FP4X4),
                        rhs_scale=sk_s[:, first + i0 : first + i0 + P],
                        start=(i0 == 0 and (c == 2 or m % 2 == 0)), stop=False,
                    )

        def u_pass(c, m, a):
            nc.tensor.matmul_mx(
                place(c, m), lhsT=wo_w[:, a, m * P : (m + 1) * P].bitcast(FP8X4),
                lhsT_scale=wo_s[:, a * N + m * P : a * N + (m + 1) * P],
                rhs=codes[c, a].bitcast(FP8X4), rhs_scale=scales[c, a],
                start=False, stop=(a == 1 and (c == 2 or m % 2 == 1)),
            )

        out_v = out.rearrange("(m p) i -> p m i", p=P)

        def finish_paired(c, result):
            first, width = CHUNKS[c]
            for m in range(4):
                u_pass(c, m, 1)
            for b in range(2):
                half = result[:, 2 * b * width : 2 * (b + 1) * width]
                nc.scalar.copy(half, banks[2 * c + b][:, : 2 * width])
                nc.sync.dma_start(
                    out_v[:, 2 * b : 2 * b + 2, first : first + width], half.rearrange("p (m i) -> p m i", m=2)
                )

        def own(name, dtype, width):
            return keep.tile([P, width], dtype, name=name, align_bytes=64)[:]

        def shared(name, dtype, width, offset):
            return turns.tile([P, width], dtype, name=name, align_bytes=64, offset=offset)[:]

        for c in range(3):
            skip_passes(c)

        picked_a, woven_a = own("picked_a", F32, 1024), own("woven_a", BF16, 1024)
        pick(0, 0, 256, picked_a)
        scale_and_weave(0, 256, picked_a, shared("rows_a", BF16, 1024, 4096), woven_a)
        picked_b, woven_b = own("picked_b", F32, 1024), own("woven_b", BF16, 1024)
        pick(1, 0, 256, picked_b)
        scale_and_weave(1, 256, picked_b, shared("rows_b", BF16, 1024, 5120), woven_b)
        quantise(0, 0, 256, woven_a)
        for m in range(4):
            u_pass(0, m, 0)

        picked_c, woven_c = shared("picked_c", F32, 1024, 256), own("woven_c", BF16, 1024)
        pick(0, 256, 256, picked_c)
        scale_and_weave(0, 256, picked_c, shared("rows_c", BF16, 1024, 6400), woven_c)
        quantise(1, 0, 256, woven_b)

        picked_d, woven_d = shared("picked_d", F32, 512, 4352), own("woven_d", BF16, 512)
        pick(1, 256, 128, picked_d)
        scale_and_weave(1, 128, picked_d, shared("rows_d", BF16, 512, 6400), woven_d)
        quantise(0, 256, 256, woven_c)
        finish_paired(0, shared("result0", F32, 1024, 2816))
        for c in (1, 2):
            for m in range(4):
                u_pass(c, m, 0)

        picked_e = shared("picked_e", F32, 512, 7936)
        pick(1, 384, 128, picked_e)
        quantise(1, 256, 128, woven_d)
        finish_paired(1, own("result1", F32, 512))
        woven_e = shared("woven_e", BF16, 512, 6912)
        nc.vector.tensor_tensor(
            woven_e.rearrange("p (g i s) -> p g s i", i=2, s=4), picked_e.rearrange("p (s g i) -> p g s i", s=4, i=2),
            factor[:, 1, :].unsqueeze(1).unsqueeze(3).to_broadcast([P, 64, 4, 2]), MULT,
        )
        quantise(1, 384, 128, woven_e)
        first, width = CHUNKS[2]
        for pair in range(2):
            result = keep.tile([P, 2, width], F32, name=f"result2_{pair}")
            for m in (2 * pair, 2 * pair + 1):
                u_pass(2, m, 1)
            nc.scalar.copy(result[:, 0, :], place(2, 2 * pair))
            nc.vector.tensor_copy(result[:, 1, :], place(2, 2 * pair + 1))
            queue = nc.sync if pair == 0 else nc.scalar
            queue.dma_start(out_v[:, 2 * pair : 2 * pair + 2, first : first + width], result[:])
